import numpy as np
import ml_dtypes


def mxq(x, axis, fmt="e4m3"):
    dtype, down = {"e4m3": (ml_dtypes.float8_e4m3fn, 7), "e5m2": (ml_dtypes.float8_e5m2, 14)}[fmt]
    v = np.moveaxis(np.asarray(x, np.float32).astype(ml_dtypes.bfloat16).astype(np.float64), axis, -1)
    blocks = v.reshape(v.shape[:-1] + (-1, 32))
    amax = np.abs(blocks).max(-1, keepdims=True)
    byte = np.maximum(np.where(amax > 0, np.frexp(amax)[1] - 1 + 127, 0) - down, 1)
    scale = np.exp2(byte - 127.0)
    codes = (blocks / scale).astype(np.float32).astype(dtype).astype(np.float64)
    return np.moveaxis((codes * scale).reshape(v.shape), -1, axis)


WIDE = False


def mx_kscale(k):
    if not WIDE:
        return np.ones(k)
    levels = np.array([10, -10, 5, -5, 0])
    if k % 512:
        return np.exp2(np.random.permutation(np.resize(levels, k // 32))).repeat(32)
    a = np.empty((k // 512, 16))
    for p in range(k // 512):
        a[p, :8] = np.random.permutation(np.resize(levels, 8))
        for g in range(8):
            far = levels[np.abs(levels - a[p, g]) >= 10]
            a[p, g + 8] = far[np.random.randint(len(far))]
    return np.exp2(a.ravel()).repeat(32)


def f64(x):
    return np.asarray(x).astype(np.float64)


def striped(idx):
    return np.tile(np.asarray(idx).reshape(-1, 16).T, (8, 1)).astype(np.uint16)


def unstriped(offs):
    return offs[:16].T.reshape(-1).astype(np.int64)


E2M1 = np.array([0.0, 0.5, 1.0, 1.5, 2.0, 3.0, 4.0, 6.0, -0.0, -0.5, -1.0, -1.5, -2.0, -3.0, -4.0, -6.0])


def pack_weight(w, fmt):
    k, n = w.shape
    w = f64(np.asarray(w, np.float32).astype(ml_dtypes.bfloat16)).reshape(k // 32, 32, n)
    amax = np.abs(w).max(1)
    if fmt == "e4m3":
        byte = np.frexp(amax)[1] - 1 + 127 - 7
    else:
        mant, ex = np.frexp(amax / 6.0)
        byte = np.where(mant > 0.5, ex, ex - 1) + 127
    byte = np.clip(np.where(amax > 0, byte, 1), 1, 254)
    scaled = (w * np.exp2(127.0 - byte)[:, None, :]).reshape(k, n).astype(np.float32)
    by_word = np.ascontiguousarray(scaled.reshape(k // 512, 128, 4, n).transpose(0, 1, 3, 2))
    if fmt == "e4m3":
        words = by_word.astype(ml_dtypes.float8_e4m3fn).view(np.uint8)
    else:
        c = by_word.astype(ml_dtypes.float4_e2m1fn).view(np.uint8) & 0xF
        words = (c[..., 0::2] | (c[..., 1::2] << 4)).reshape(k // 512, 128, 2 * n)
    return np.ascontiguousarray(words), np.ascontiguousarray(byte.astype(np.uint8).reshape(k // 512, 16, n))


def unpack_weight(words, scales, fmt):
    g, _, n = scales.shape
    words = np.ascontiguousarray(words).reshape(g, 128, n, -1)
    if fmt == "e4m3":
        vals = words.view(ml_dtypes.float8_e4m3fn).astype(np.float64)
    else:
        nib = np.empty((g, 128, n, 4), np.uint8)
        nib[..., 0::2] = words & 0xF
        nib[..., 1::2] = words >> 4
        vals = E2M1[nib]
    vals = vals * np.repeat(np.exp2(scales.astype(np.float64) - 127.0), 8, axis=1)[..., None]
    return vals.transpose(0, 1, 3, 2).reshape(g * 512, n)


D, K, T, M, I, E = 512, 512, 2048, 1024, 512, 256


def setup_inputs():
    n = np.random.standard_normal
    idx = np.random.permutation(T)[:I]
    idx2 = np.random.permutation(M)[:I]
    idx3 = np.random.permutation(M)[:I]
    fd = mx_kscale(D)
    fk = mx_kscale(K)
    pagesp = pack_weight(n((D, T)) / fd[:, None], "e2m1")
    wap = pack_weight(n((D, K)) * 1.0 / np.sqrt(D) * fd[:, None], "e4m3")
    wop = pack_weight(n((K, E)) * 1.0 / np.sqrt(K) / fk[:, None], "e4m3")
    return {
        "pages_words": pagesp[0],
        "pages_scales": pagesp[1],
        "wa_words": wap[0],
        "wa_scales": wap[1],
        "kf": (np.random.uniform(0.5, 2.0, (K, 1)) * fk[:, None]).astype(np.float32),
        "wo_words": wop[0],
        "wo_scales": wop[1],
        "offs": striped(idx),
        "offs2": striped(idx2),
        "offs3": striped(idx3),
    }


def reference(pages_words, pages_scales, wa_words, wa_scales, kf, wo_words, wo_scales, offs, offs2, offs3):
    idx = unstriped(offs)
    idx2 = unstriped(offs2)
    idx3 = unstriped(offs3)
    pagesu = unpack_weight(pages_words, pages_scales, "e2m1")
    wau = unpack_weight(wa_words, wa_scales, "e4m3")
    wou = unpack_weight(wo_words, wo_scales, "e4m3")
    pagesidxg = pagesu[:, idx]
    z = wau.T @ pagesidxg
    f1 = np.zeros((K, M))
    f1[:, idx2] = z
    v = f1[:, idx3] - z
    w = v * f64(kf)
    wq = mxq(w, 0, "e4m3")
    y = wou.T @ wq
    return y

@@ -1,0 +1,169 @@
+from contextlib import ExitStack
+
+import concourse.mybir as mybir
+
+D, K, T, M, I, E = 512, 512, 2048, 1024, 512, 256
+FLOPS = 2 * D * K * I + 2 * K * E * I
+
+F32 = mybir.dt.float32
+BF16 = mybir.dt.bfloat16
+I32 = mybir.dt.int32
+U32 = mybir.dt.uint32
+U16 = mybir.dt.uint16
+U8 = mybir.dt.uint8
+FP8X4 = mybir.dt.float8_e4m3fn_x4
+FP4X4 = mybir.dt.float4_e2m1fn_x4
+COPY = mybir.ActivationFunctionType.Copy
+MULT = mybir.AluOpType.mult
+SUBTRACT = mybir.AluOpType.subtract
+
+P = 128
+PACK = 4
+HALF = I // 2
+PER_COLUMN = 16
+
+
+def tile_attend_pagerelay_kernel(tc, pages_words, pages_scales, wa_words, wa_scales, kf, wo_words, wo_scales, offs, offs2, offs3, out):
+    nc = tc.nc
+    with ExitStack() as ctx:
+        sb = ctx.enter_context(tc.tile_pool(name="sb", bufs=1))
+        psum = ctx.enter_context(tc.psum_pool(name="psum", bufs=1))
+
+        def slots(h):
+            return slice(h * HALF, (h + 1) * HALF)
+
+        def entries(h):
+            return slice(h * HALF // PER_COLUMN, (h + 1) * HALF // PER_COLUMN)
+
+        def load_scale_rows(plane, rows, queues):
+            for q in range(4):
+                queues[q].dma_start(plane[32 * q : 32 * q + 4, :].bitcast(I32), rows[0, 4 * q : 4 * q + 4, :].bitcast(I32))
+
+        page_list = sb.tile([P, I // PER_COLUMN], U16, name="page_list")
+        put_list = sb.tile([P, I // PER_COLUMN], U16, name="put_list")
+        get_list = sb.tile([P, I // PER_COLUMN], U16, name="get_list")
+        pages_w = sb.tile([P, T], U16, name="pages_w", align_bytes=64)
+        pages_s = sb.tile([P, T], U8, name="pages_s", align_bytes=64)
+        wa_w = sb.tile([P, K], U32, name="wa_w", align_bytes=64)
+        wa_s = sb.tile([P, K], U8, name="wa_s", align_bytes=64)
+        wo_w = wa_w[:, 0:E]
+        wo_s = wa_s[:, 0:E]
+        factors = sb.tile([P, PACK], F32, name="factors")
+        f1 = [sb.tile([P, M], F32, name=f"f1_{t}", align_bytes=64) for t in range(PACK)]
+
+        for plane in (wa_s, pages_s):
+            nc.vector.memset(plane[:].bitcast(I32), 0)
+        for t in range(PACK):
+            nc.vector.memset(f1[t][:].bitcast(I32), 0)
+
+        nc.sync.dma_start(page_list[:], offs)
+        nc.sync.dma_start(wa_w[:].bitcast(I32), wa_words[0].rearrange("p n t -> p (n t)").bitcast(I32))
+        nc.sync.dma_start(pages_w[:].bitcast(I32), pages_words[0].bitcast(I32))
+        load_scale_rows(wa_s, wa_scales, [nc.sync] * 3 + [nc.gpsimd])
+        load_scale_rows(pages_s, pages_scales, [nc.sync] * 4)
+        nc.sync.dma_start(put_list[:], offs2)
+        nc.sync.dma_start(get_list[:], offs3)
+        nc.gpsimd.dma_start(factors[:], kf.rearrange("(p t) o -> p (t o)", t=PACK))
+
+        dealt_w = sb.tile([P, PACK, P], U32, name="dealt_w", align_bytes=64)
+        dealt_s = sb.tile([P, PACK, P], U8, name="dealt_s", align_bytes=64)
+        nc.gpsimd.tensor_copy(dealt_w[:], wa_w[:].rearrange("p (m t) -> p t m", t=PACK))
+        nc.gpsimd.tensor_copy(dealt_s[:], wa_s[:].rearrange("p (m t) -> p t m", t=PACK))
+        nc.sync.dma_start(wo_w.bitcast(I32), wo_words[0].rearrange("p n t -> p (n t)").bitcast(I32))
+        load_scale_rows(wo_s, wo_scales, [nc.sync] * 4)
+
+        LAST = PACK - 1
+        z = sb.tile([P, PACK, I], F32, name="z", align_bytes=64)
+        picked_w = sb.tile([P, I], U16, name="picked_w", align_bytes=64)
+        nc.vector.tensor_copy(picked_w[:], pages_w[:].indirect(page_list[:]))
+        bank_groups = [(0, [0]), (0, [1]), (0, [2, 3]), (1, [0, 1]), (1, [2, 3])]
+        picked_s = []
+        for h in range(2):
+            tile = sb.tile([P, HALF], U8, name=f"picked_s{h}", align_bytes=64)
+            nc.vector.tensor_copy(tile[:], pages_s[:].indirect(page_list[:, entries(h)]))
+            picked_s.append(tile)
+        z_banks = []
+        for n, (h, ts) in enumerate(bank_groups):
+            bank = psum.tile([P, len(ts), HALF], F32, name=f"z_bank{n}")
+            for j, t in enumerate(ts):
+                nc.tensor.matmul_mx(
+                    bank[:, j, :],
+                    lhsT=dealt_w[:, t, :].bitcast(FP8X4),
+                    lhsT_scale=dealt_s[:, t, :],
+                    rhs=picked_w[:, slots(h)].bitcast(FP4X4),
+                    rhs_scale=picked_s[h][:],
+                    start=True,
+                    stop=True,
+                )
+            z_banks.append(bank)
+
+        def copy_on(engine, dst, src):
+            if engine == "vector":
+                nc.vector.tensor_copy(dst, src)
+            else:
+                nc.scalar.activation(dst, src, COPY)
+
+        def copy_z(engine, n):
+            h, ts = bank_groups[n]
+            copy_on(engine, z[:, ts[0] : ts[-1] + 1, slots(h)], z_banks[n][:])
+
+        def put(engine, t, h):
+            copy_on(engine, f1[t][:].indirect(put_list[:, entries(h)]), z[:, t, slots(h)])
+
+        v = sb.tile([P, LAST, I], F32, name="v", align_bytes=64)
+
+        copy_z("vector", 0)
+        copy_z("scalar", 1)
+        put("vector", 0, 0)
+        put("scalar", 1, 0)
+        copy_z("vector", 3)
+        copy_z("vector", 2)
+        put("vector", 0, 1)
+        put("scalar", 1, 1)
+        copy_z("scalar", 4)
+        for t in range(2, PACK):
+            put("scalar", t, 1)
+            put("scalar", t, 0)
+        for t in range(LAST):
+            nc.vector.tensor_tensor(v[:, t, :], f1[t][:].indirect(get_list[:]), z[:, t, :], SUBTRACT)
+
+        woven = [sb.tile([P, HALF, PACK], BF16, name=f"woven{h}", align_bytes=64) for h in range(2)]
+        run = 4
+        spread = factors[:, 0:LAST].unsqueeze(1).unsqueeze(3).broadcast_to([P, HALF // run, LAST, run])
+        for h in range(2):
+            nc.vector.tensor_tensor(
+                woven[h][:, :, 0:LAST].rearrange("p (c i) t -> p c t i", i=run),
+                v[:, :, slots(h)].rearrange("p t (c i) -> p c t i", i=run),
+                spread,
+                MULT,
+            )
+
+        v_last = v[:, 0, :]
+        found = sb.tile([P, HALF], F32, name="found", align_bytes=64)
+        nc.vector.tensor_tensor(v_last[:, slots(0)], f1[LAST][:].indirect(get_list[:, entries(0)]), z[:, LAST, slots(0)], SUBTRACT)
+        nc.scalar.activation(found[:], f1[LAST][:].indirect(get_list[:, entries(1)]), COPY)
+        nc.vector.tensor_tensor(v_last[:, slots(1)], found[:], z[:, LAST, slots(1)], SUBTRACT)
+        for h in range(2):
+            nc.vector.tensor_scalar(woven[h][:, :, LAST], v_last[:, slots(h)], factors[:, LAST : LAST + 1], None, MULT)
+
+        out_rows = out.rearrange("(e p) i -> p e i", p=P)
+        for h in range(2):
+            codes = sb.tile([P, HALF], U32, name=f"codes{h}", align_bytes=64)
+            code_s = sb.tile([P, HALF], U8, name=f"code_s{h}", align_bytes=64)
+            nc.vector.quantize_mx(codes[:].bitcast(FP8X4), code_s[:], woven[h][:].rearrange("p i t -> p (i t)"))
+            groups = [[0, 1]] if h == 0 else [[0], [1]]
+            for es in groups:
+                bank = psum.tile([P, len(es), HALF], F32, name=f"y_bank{h}{es[0]}")
+                for j, e in enumerate(es):
+                    nc.tensor.matmul_mx(
+                        bank[:, j, :],
+                        lhsT=wo_w[:, e * P : (e + 1) * P].bitcast(FP8X4),
+                        lhsT_scale=wo_s[:, e * P : (e + 1) * P],
+                        rhs=codes[:].bitcast(FP8X4),
+                        rhs_scale=code_s[:],
+                        start=True,
+                        stop=True,
+                    )
+                y = sb.tile([P, len(es), HALF], F32, name=f"y{h}{es[0]}", align_bytes=64)
+                copy_on("vector" if h == 1 and es == [0] else "scalar", y[:], bank[:])
+                nc.sync.dma_start(out_rows[:, es[0] : es[-1] + 1, slots(h)], y[:])

@@ -51,47 +51,46 @@ def tile_attend_pagerelay_kernel(tc, pages_words, pages_scales, wa_words, wa_sca
         factors = sb.tile([P, PACK], F32, name="factors")
         f1 = [sb.tile([P, M], F32, name=f"f1_{t}", align_bytes=64) for t in range(PACK)]
 
-        for plane in (wa_s, pages_s):
+        for plane in (pages_s, wa_s):
             nc.vector.memset(plane[:].bitcast(I32), 0)
         for t in range(PACK):
             nc.vector.memset(f1[t][:].bitcast(I32), 0)
 
+        nc.sync.dma_start(pages_w[:].bitcast(I32), pages_words[0].bitcast(I32))
         nc.sync.dma_start(page_list[:], offs)
         nc.sync.dma_start(wa_w[:].bitcast(I32), wa_words[0].rearrange("p n t -> p (n t)").bitcast(I32))
-        nc.sync.dma_start(pages_w[:].bitcast(I32), pages_words[0].bitcast(I32))
-        load_scale_rows(wa_s, wa_scales, [nc.sync] * 3 + [nc.gpsimd])
         load_scale_rows(pages_s, pages_scales, [nc.sync] * 4)
+        load_scale_rows(wa_s, wa_scales, [nc.sync] * 4)
         nc.sync.dma_start(put_list[:], offs2)
         nc.sync.dma_start(get_list[:], offs3)
         nc.gpsimd.dma_start(factors[:], kf.rearrange("(p t) o -> p (t o)", t=PACK))
 
         dealt_w = sb.tile([P, PACK, P], U32, name="dealt_w", align_bytes=64)
         dealt_s = sb.tile([P, PACK, P], U8, name="dealt_s", align_bytes=64)
-        nc.gpsimd.tensor_copy(dealt_w[:], wa_w[:].rearrange("p (m t) -> p t m", t=PACK))
-        nc.gpsimd.tensor_copy(dealt_s[:], wa_s[:].rearrange("p (m t) -> p t m", t=PACK))
-        nc.sync.dma_start(wo_w.bitcast(I32), wo_words[0].rearrange("p n t -> p (n t)").bitcast(I32))
-        load_scale_rows(wo_s, wo_scales, [nc.sync] * 4)
-
         LAST = PACK - 1
         z = sb.tile([P, PACK, I], F32, name="z", align_bytes=64)
         picked_w = sb.tile([P, I], U16, name="picked_w", align_bytes=64)
         nc.vector.tensor_copy(picked_w[:], pages_w[:].indirect(page_list[:]))
-        bank_groups = [(0, [0]), (0, [1]), (0, [2, 3]), (1, [0, 1]), (1, [2, 3])]
-        picked_s = []
-        for h in range(2):
-            tile = sb.tile([P, HALF], U8, name=f"picked_s{h}", align_bytes=64)
-            nc.vector.tensor_copy(tile[:], pages_s[:].indirect(page_list[:, entries(h)]))
-            picked_s.append(tile)
+        nc.vector.tensor_copy(dealt_w[:], wa_w[:].rearrange("p (m t) -> p t m", t=PACK))
+        nc.sync.dma_start(wo_w.bitcast(I32), wo_words[0].rearrange("p n t -> p (n t)").bitcast(I32))
+        picked_s = sb.tile([P, I], U8, name="picked_s", align_bytes=64)
+        nc.vector.tensor_copy(picked_s[:], pages_s[:].indirect(page_list[:]))
+        for u in range(2):
+            nc.vector.tensor_copy(dealt_s[:, 2 * u : 2 * u + 2, :], wa_s[:].rearrange("p (m t) -> p t m", t=PACK)[:, 2 * u : 2 * u + 2, :])
+        load_scale_rows(wo_s, wo_scales, [nc.sync] * 4)
+
+        every = slice(0, I)
+        bank_groups = [([0], slots(0)), ([1], slots(0)), ([0, 1], slots(1)), ([2], every), ([3], every)]
         z_banks = []
-        for n, (h, ts) in enumerate(bank_groups):
-            bank = psum.tile([P, len(ts), HALF], F32, name=f"z_bank{n}")
+        for n, (ts, cols) in enumerate(bank_groups):
+            bank = psum.tile([P, len(ts), cols.stop - cols.start], F32, name=f"z_bank{n}")
             for j, t in enumerate(ts):
                 nc.tensor.matmul_mx(
                     bank[:, j, :],
                     lhsT=dealt_w[:, t, :].bitcast(FP8X4),
                     lhsT_scale=dealt_s[:, t, :],
-                    rhs=picked_w[:, slots(h)].bitcast(FP4X4),
-                    rhs_scale=picked_s[h][:],
+                    rhs=picked_w[:, cols].bitcast(FP4X4),
+                    rhs_scale=picked_s[:, cols],
                     start=True,
                     stop=True,
                 )
@@ -104,8 +103,8 @@ def tile_attend_pagerelay_kernel(tc, pages_words, pages_scales, wa_words, wa_sca
                 nc.scalar.activation(dst, src, COPY)
 
         def copy_z(engine, n):
-            h, ts = bank_groups[n]
-            copy_on(engine, z[:, ts[0] : ts[-1] + 1, slots(h)], z_banks[n][:])
+            ts, cols = bank_groups[n]
+            copy_on(engine, z[:, ts[0] : ts[-1] + 1, cols], z_banks[n][:])
 
         def put(engine, t, h):
             copy_on(engine, f1[t][:].indirect(put_list[:, entries(h)]), z[:, t, slots(h)])
@@ -116,14 +115,14 @@ def tile_attend_pagerelay_kernel(tc, pages_words, pages_scales, wa_words, wa_sca
         copy_z("scalar", 1)
         put("vector", 0, 0)
         put("scalar", 1, 0)
-        copy_z("vector", 3)
         copy_z("vector", 2)
+        copy_z("scalar", 3)
         put("vector", 0, 1)
         put("scalar", 1, 1)
-        copy_z("scalar", 4)
+        copy_z("vector", 4)
         for t in range(2, PACK):
-            put("scalar", t, 1)
             put("scalar", t, 0)
+            put("scalar", t, 1)
         for t in range(LAST):
             nc.vector.tensor_tensor(v[:, t, :], f1[t][:].indirect(get_list[:]), z[:, t, :], SUBTRACT)
 
@@ -143,8 +142,8 @@ def tile_attend_pagerelay_kernel(tc, pages_words, pages_scales, wa_words, wa_sca
         nc.vector.tensor_tensor(v_last[:, slots(0)], f1[LAST][:].indirect(get_list[:, entries(0)]), z[:, LAST, slots(0)], SUBTRACT)
         nc.scalar.activation(found[:], f1[LAST][:].indirect(get_list[:, entries(1)]), COPY)
         nc.vector.tensor_tensor(v_last[:, slots(1)], found[:], z[:, LAST, slots(1)], SUBTRACT)
-        for h in range(2):
-            nc.vector.tensor_scalar(woven[h][:, :, LAST], v_last[:, slots(h)], factors[:, LAST : LAST + 1], None, MULT)
+        nc.vector.tensor_scalar(woven[0][:, :, LAST], v_last[:, slots(0)], factors[:, LAST : LAST + 1], None, MULT)
+        nc.scalar.activation(woven[1][:, :, LAST], v_last[:, slots(1)], COPY, scale=factors[:, LAST : LAST + 1])
 
         out_rows = out.rearrange("(e p) i -> p e i", p=P)
         for h in range(2):

from contextlib import ExitStack

import concourse.mybir as mybir

D, K, T, M, I, E = 512, 512, 2048, 1024, 512, 256
FLOPS = 2 * D * K * I + 2 * K * E * I

F32 = mybir.dt.float32
BF16 = mybir.dt.bfloat16
I32 = mybir.dt.int32
U32 = mybir.dt.uint32
U16 = mybir.dt.uint16
U8 = mybir.dt.uint8
FP8X4 = mybir.dt.float8_e4m3fn_x4
FP4X4 = mybir.dt.float4_e2m1fn_x4
COPY = mybir.ActivationFunctionType.Copy
MULT = mybir.AluOpType.mult
SUBTRACT = mybir.AluOpType.subtract

P = 128
PACK = 4
HALF = I // 2
PER_COLUMN = 16


def tile_attend_pagerelay_kernel(tc, pages_words, pages_scales, wa_words, wa_scales, kf, wo_words, wo_scales, offs, offs2, offs3, out):
    nc = tc.nc
    with ExitStack() as ctx:
        sb = ctx.enter_context(tc.tile_pool(name="sb", bufs=1))
        psum = ctx.enter_context(tc.psum_pool(name="psum", bufs=1))

        def slots(h):
            return slice(h * HALF, (h + 1) * HALF)

        def entries(h):
            return slice(h * HALF // PER_COLUMN, (h + 1) * HALF // PER_COLUMN)

        def load_scale_rows(plane, rows, queues):
            for q in range(4):
                queues[q].dma_start(plane[32 * q : 32 * q + 4, :].bitcast(I32), rows[0, 4 * q : 4 * q + 4, :].bitcast(I32))

        page_list = sb.tile([P, I // PER_COLUMN], U16, name="page_list")
        put_list = sb.tile([P, I // PER_COLUMN], U16, name="put_list")
        get_list = sb.tile([P, I // PER_COLUMN], U16, name="get_list")
        pages_w = sb.tile([P, T], U16, name="pages_w", align_bytes=64)
        pages_s = sb.tile([P, T], U8, name="pages_s", align_bytes=64)
        wa_w = sb.tile([P, K], U32, name="wa_w", align_bytes=64)
        wa_s = sb.tile([P, K], U8, name="wa_s", align_bytes=64)
        wo_w = wa_w[:, 0:E]
        wo_s = wa_s[:, 0:E]
        factors = sb.tile([P, PACK], F32, name="factors")
        f1 = [sb.tile([P, M], F32, name=f"f1_{t}", align_bytes=64) for t in range(PACK)]

        for plane in (pages_s, wa_s):
            nc.vector.memset(plane[:].bitcast(I32), 0)
        for t in range(PACK):
            nc.vector.memset(f1[t][:].bitcast(I32), 0)

        nc.sync.dma_start(pages_w[:].bitcast(I32), pages_words[0].bitcast(I32))
        nc.sync.dma_start(page_list[:], offs)
        nc.sync.dma_start(wa_w[:].bitcast(I32), wa_words[0].rearrange("p n t -> p (n t)").bitcast(I32))
        load_scale_rows(pages_s, pages_scales, [nc.sync] * 4)
        load_scale_rows(wa_s, wa_scales, [nc.sync] * 4)
        nc.sync.dma_start(put_list[:], offs2)
        nc.sync.dma_start(get_list[:], offs3)
        nc.gpsimd.dma_start(factors[:], kf.rearrange("(p t) o -> p (t o)", t=PACK))

        dealt_w = sb.tile([P, PACK, P], U32, name="dealt_w", align_bytes=64)
        dealt_s = sb.tile([P, PACK, P], U8, name="dealt_s", align_bytes=64)
        LAST = PACK - 1
        z = sb.tile([P, PACK, I], F32, name="z", align_bytes=64)
        picked_w = sb.tile([P, I], U16, name="picked_w", align_bytes=64)
        nc.vector.tensor_copy(picked_w[:], pages_w[:].indirect(page_list[:]))
        nc.vector.tensor_copy(dealt_w[:], wa_w[:].rearrange("p (m t) -> p t m", t=PACK))
        nc.sync.dma_start(wo_w.bitcast(I32), wo_words[0].rearrange("p n t -> p (n t)").bitcast(I32))
        picked_s = sb.tile([P, I], U8, name="picked_s", align_bytes=64)
        nc.vector.tensor_copy(picked_s[:], pages_s[:].indirect(page_list[:]))
        for u in range(2):
            nc.vector.tensor_copy(dealt_s[:, 2 * u : 2 * u + 2, :], wa_s[:].rearrange("p (m t) -> p t m", t=PACK)[:, 2 * u : 2 * u + 2, :])
        load_scale_rows(wo_s, wo_scales, [nc.sync] * 4)

        every = slice(0, I)
        bank_groups = [([0], slots(0)), ([1], slots(0)), ([0, 1], slots(1)), ([2], every), ([3], every)]
        z_banks = []
        for n, (ts, cols) in enumerate(bank_groups):
            bank = psum.tile([P, len(ts), cols.stop - cols.start], F32, name=f"z_bank{n}")
            for j, t in enumerate(ts):
                nc.tensor.matmul_mx(
                    bank[:, j, :],
                    lhsT=dealt_w[:, t, :].bitcast(FP8X4),
                    lhsT_scale=dealt_s[:, t, :],
                    rhs=picked_w[:, cols].bitcast(FP4X4),
                    rhs_scale=picked_s[:, cols],
                    start=True,
                    stop=True,
                )
            z_banks.append(bank)

        def copy_on(engine, dst, src):
            if engine == "vector":
                nc.vector.tensor_copy(dst, src)
            else:
                nc.scalar.activation(dst, src, COPY)

        def copy_z(engine, n):
            ts, cols = bank_groups[n]
            copy_on(engine, z[:, ts[0] : ts[-1] + 1, cols], z_banks[n][:])

        def put(engine, t, h):
            copy_on(engine, f1[t][:].indirect(put_list[:, entries(h)]), z[:, t, slots(h)])

        v = sb.tile([P, LAST, I], F32, name="v", align_bytes=64)

        copy_z("vector", 0)
        copy_z("scalar", 1)
        put("vector", 0, 0)
        put("scalar", 1, 0)
        copy_z("vector", 2)
        copy_z("scalar", 3)
        put("vector", 0, 1)
        put("scalar", 1, 1)
        copy_z("vector", 4)
        for t in range(2, PACK):
            put("scalar", t, 0)
            put("scalar", t, 1)
        for t in range(LAST):
            nc.vector.tensor_tensor(v[:, t, :], f1[t][:].indirect(get_list[:]), z[:, t, :], SUBTRACT)

        woven = [sb.tile([P, HALF, PACK], BF16, name=f"woven{h}", align_bytes=64) for h in range(2)]
        run = 4
        spread = factors[:, 0:LAST].unsqueeze(1).unsqueeze(3).broadcast_to([P, HALF // run, LAST, run])
        for h in range(2):
            nc.vector.tensor_tensor(
                woven[h][:, :, 0:LAST].rearrange("p (c i) t -> p c t i", i=run),
                v[:, :, slots(h)].rearrange("p t (c i) -> p c t i", i=run),
                spread,
                MULT,
            )

        v_last = v[:, 0, :]
        found = sb.tile([P, HALF], F32, name="found", align_bytes=64)
        nc.vector.tensor_tensor(v_last[:, slots(0)], f1[LAST][:].indirect(get_list[:, entries(0)]), z[:, LAST, slots(0)], SUBTRACT)
        nc.scalar.activation(found[:], f1[LAST][:].indirect(get_list[:, entries(1)]), COPY)
        nc.vector.tensor_tensor(v_last[:, slots(1)], found[:], z[:, LAST, slots(1)], SUBTRACT)
        nc.vector.tensor_scalar(woven[0][:, :, LAST], v_last[:, slots(0)], factors[:, LAST : LAST + 1], None, MULT)
        nc.scalar.activation(woven[1][:, :, LAST], v_last[:, slots(1)], COPY, scale=factors[:, LAST : LAST + 1])

        out_rows = out.rearrange("(e p) i -> p e i", p=P)
        for h in range(2):
            codes = sb.tile([P, HALF], U32, name=f"codes{h}", align_bytes=64)
            code_s = sb.tile([P, HALF], U8, name=f"code_s{h}", align_bytes=64)
            nc.vector.quantize_mx(codes[:].bitcast(FP8X4), code_s[:], woven[h][:].rearrange("p i t -> p (i t)"))
            groups = [[0, 1]] if h == 0 else [[0], [1]]
            for es in groups:
                bank = psum.tile([P, len(es), HALF], F32, name=f"y_bank{h}{es[0]}")
                for j, e in enumerate(es):
                    nc.tensor.matmul_mx(
                        bank[:, j, :],
                        lhsT=wo_w[:, e * P : (e + 1) * P].bitcast(FP8X4),
                        lhsT_scale=wo_s[:, e * P : (e + 1) * P],
                        rhs=codes[:].bitcast(FP8X4),
                        rhs_scale=code_s[:],
                        start=True,
                        stop=True,
                    )
                y = sb.tile([P, len(es), HALF], F32, name=f"y{h}{es[0]}", align_bytes=64)
                copy_on("vector" if h == 1 and es == [0] else "scalar", y[:], bank[:])
                nc.sync.dma_start(out_rows[:, es[0] : es[-1] + 1, slots(h)], y[:])
